import numpy as np
import ml_dtypes


def mxq(x, axis, fmt="e4m3"):
    dtype, down = {"e4m3": (ml_dtypes.float8_e4m3fn, 7), "e5m2": (ml_dtypes.float8_e5m2, 14)}[fmt]
    v = np.moveaxis(np.asarray(x, np.float32).astype(ml_dtypes.bfloat16).astype(np.float64), axis, -1)
    blocks = v.reshape(v.shape[:-1] + (-1, 32))
    amax = np.abs(blocks).max(-1, keepdims=True)
    byte = np.maximum(np.where(amax > 0, np.frexp(amax)[1] - 1 + 127, 0) - down, 1)
    scale = np.exp2(byte - 127.0)
    codes = (blocks / scale).astype(np.float32).astype(dtype).astype(np.float64)
    return np.moveaxis((codes * scale).reshape(v.shape), -1, axis)


WIDE = False


def mx_kscale(k):
    if not WIDE:
        return np.ones(k)
    levels = np.array([10, -10, 5, -5, 0])
    if k % 512:
        return np.exp2(np.random.permutation(np.resize(levels, k // 32))).repeat(32)
    a = np.empty((k // 512, 16))
    for p in range(k // 512):
        a[p, :8] = np.random.permutation(np.resize(levels, 8))
        for g in range(8):
            far = levels[np.abs(levels - a[p, g]) >= 10]
            a[p, g + 8] = far[np.random.randint(len(far))]
    return np.exp2(a.ravel()).repeat(32)


def f64(x):
    return np.asarray(x).astype(np.float64)


def striped(idx):
    return np.tile(np.asarray(idx).reshape(-1, 16).T, (8, 1)).astype(np.uint16)


def unstriped(offs):
    return offs[:16].T.reshape(-1).astype(np.int64)


E2M1 = np.array([0.0, 0.5, 1.0, 1.5, 2.0, 3.0, 4.0, 6.0, -0.0, -0.5, -1.0, -1.5, -2.0, -3.0, -4.0, -6.0])


def pack_weight(w, fmt):
    k, n = w.shape
    w = f64(np.asarray(w, np.float32).astype(ml_dtypes.bfloat16)).reshape(k // 32, 32, n)
    amax = np.abs(w).max(1)
    if fmt == "e4m3":
        byte = np.frexp(amax)[1] - 1 + 127 - 7
    else:
        mant, ex = np.frexp(amax / 6.0)
        byte = np.where(mant > 0.5, ex, ex - 1) + 127
    byte = np.clip(np.where(amax > 0, byte, 1), 1, 254)
    scaled = (w * np.exp2(127.0 - byte)[:, None, :]).reshape(k, n).astype(np.float32)
    by_word = np.ascontiguousarray(scaled.reshape(k // 512, 128, 4, n).transpose(0, 1, 3, 2))
    if fmt == "e4m3":
        words = by_word.astype(ml_dtypes.float8_e4m3fn).view(np.uint8)
    else:
        c = by_word.astype(ml_dtypes.float4_e2m1fn).view(np.uint8) & 0xF
        words = (c[..., 0::2] | (c[..., 1::2] << 4)).reshape(k // 512, 128, 2 * n)
    return np.ascontiguousarray(words), np.ascontiguousarray(byte.astype(np.uint8).reshape(k // 512, 16, n))


def unpack_weight(words, scales, fmt):
    g, _, n = scales.shape
    words = np.ascontiguousarray(words).reshape(g, 128, n, -1)
    if fmt == "e4m3":
        vals = words.view(ml_dtypes.float8_e4m3fn).astype(np.float64)
    else:
        nib = np.empty((g, 128, n, 4), np.uint8)
        nib[..., 0::2] = words & 0xF
        nib[..., 1::2] = words >> 4
        vals = E2M1[nib]
    vals = vals * np.repeat(np.exp2(scales.astype(np.float64) - 127.0), 8, axis=1)[..., None]
    return vals.transpose(0, 1, 3, 2).reshape(g * 512, n)


def softplus(v):
    return np.log(1.0 + np.exp(v))


def sigmoid(v):
    return 1.0 / (1.0 + np.exp(-v))


D, E, T, I, G, U, Q = 512, 512, 4096, 1024, 64, 512, 128


def setup_inputs():
    n = np.random.standard_normal
    idx = np.random.permutation(T)[:I]
    idx2 = np.random.permutation(U)[:G]
    fd = mx_kscale(D)
    fe = mx_kscale(E)
    keysp = pack_weight(n((D, T)) / fd[:, None], "e4m3")
    valsp = pack_weight(n((E, T)) / fe[:, None], "e4m3")
    return {
        "query": (n((D, Q)) * 1.0 / np.sqrt(D) * fd[:, None]).astype(np.float32),
        "keys_words": keysp[0],
        "keys_scales": keysp[1],
        "ptab": (n((Q, U)) * 0.5).astype(np.float32),
        "reserve": (np.random.uniform(50.0, 200.0, (Q, 1))).astype(np.float32),
        "gout": (n((E, Q)) * 1 / np.sqrt(E) * fe[:, None]).astype(np.float32),
        "vals_words": valsp[0],
        "vals_scales": valsp[1],
        "lam": (np.random.uniform(0.5, 1.5, (Q, 1))).astype(np.float32),
        "old": (0.5 * n((Q, U))).astype(np.float32),
        "offs": striped(idx),
        "offs2": striped(idx2),
    }


def reference(query, keys_words, keys_scales, ptab, reserve, gout, vals_words, vals_scales, lam, old, offs, offs2):
    idx = unstriped(offs)
    idx2 = unstriped(offs2)
    keysu = unpack_weight(keys_words, keys_scales, "e4m3")
    valsu = unpack_weight(vals_words, vals_scales, "e4m3")
    queryq = mxq(f64(query), 0, "e4m3")
    keysidxg = keysu[:, idx]
    a = queryq.T @ keysidxg
    tp = f64(ptab)[:, idx2] * f64(lam)
    tr1 = np.repeat(tp, I // G, axis=1)
    p = softplus(a - tr1)
    z = np.sum(p, axis=1, keepdims=True) + f64(reserve)
    goutq = mxq(f64(gout), 0, "e4m3")
    valsidxg = valsu[:, idx]
    c0 = goutq.T @ valsidxg
    dz = np.sum(p * c0, axis=1, keepdims=True) / np.square(z) * (-1.0)
    dp = 1.0 / z * c0 + dz
    dtr1 = dp * sigmoid(a - tr1) * (-1.0)
    dtp = dtr1.reshape(Q, G, I // G).sum(axis=2)
    gs = dtp * f64(lam) * 64.0
    gf = np.zeros((Q, U))
    gf[:, idx2] = gs
    y = f64(old) + gf
    return y

@@ -1,0 +1,196 @@
+from contextlib import ExitStack
+
+import concourse.mybir as mybir
+from concourse.masks import make_identity
+
+D, E, T, SLOTS, PAGES, U, Q = 512, 512, 4096, 1024, 64, 512, 128
+FLOPS = 2 * Q * SLOTS * (D + E)
+
+F32 = mybir.dt.float32
+BF16 = mybir.dt.bfloat16
+I32 = mybir.dt.int32
+U32 = mybir.dt.uint32
+U16 = mybir.dt.uint16
+U8 = mybir.dt.uint8
+FP8X4 = mybir.dt.float8_e4m3fn_x4
+ALU = mybir.AluOpType
+ACT = mybir.ActivationFunctionType
+AX = mybir.AxisListType
+
+P = 128
+PACK = 4
+HALF = 512
+PAGE = SLOTS // PAGES
+HALF_PAGES = HALF // PAGE
+RUN = 4
+RUNS = PAGE // RUN
+VALS_ROW = 4
+LN_GUARD = 2.0 ** -60
+
+
+def tile_attend_bpagefloor_kernel(tc, query, keys_words, keys_scales, ptab, reserve, gout,
+                                   vals_words, vals_scales, lam, old, offs, offs2, out):
+    nc = tc.nc
+    halves = range(SLOTS // HALF)
+    with ExitStack() as ctx:
+        sb = ctx.enter_context(tc.tile_pool(name="sb", bufs=1))
+        ps = ctx.enter_context(tc.psum_pool(name="ps", bufs=1))
+
+        def tile(shape, dtype, name, tag=None):
+            return sb.tile(shape, dtype, name=name, tag=tag or name, align_bytes=64)
+
+        slot_list = tile([P, SLOTS // 16], U16, "slot_list")
+        page_list = tile([P, PAGES // 16], U16, "page_list")
+        ks_all = tile([P, T], U8, "ks_all")
+        vs_all = tile([P, T], U8, "vs_all")
+        q_raw = tile([P, PACK, Q], F32, "q_raw", "keys")
+        g_raw = tile([P, PACK, Q], F32, "g_raw", "vals")
+        ptab_sb = tile([P, U], F32, "ptab_sb", "pages")
+        lam_sb = tile([P, 1], F32, "lam_sb")
+        reserve_sb = tile([P, 1], F32, "reserve_sb")
+        placed = tile([P, U], F32, "placed")
+        guard = tile([P, 1], F32, "guard")
+        warm = tile([P, 1], F32, "warm")
+
+        nc.vector.memset(ks_all[:].bitcast(I32), 0)
+        nc.vector.memset(vs_all[:].bitcast(I32), 0)
+        nc.gpsimd.memset(guard[:], LN_GUARD)
+        nc.scalar.activation(warm[:], guard[:], ACT.Sigmoid)
+
+        nc.sync.dma_start(slot_list[:], offs)
+        nc.sync.dma_start(q_raw[:], query.rearrange("(p j) w -> p j w", j=PACK))
+        nc.sync.dma_start(ptab_sb[:], ptab)
+        nc.sync.dma_start(g_raw[:], gout.rearrange("(p j) w -> p j w", j=PACK))
+        nc.sync.dma_start(page_list[:], offs2)
+        for r in range(4):
+            nc.sync.dma_start(ks_all[r:P:32, :].bitcast(I32), keys_scales[0, r:16:4, :].bitcast(I32))
+        for r in range(4):
+            nc.sync.dma_start(vs_all[VALS_ROW + r:P:32, :].bitcast(I32), vals_scales[0, r:16:4, :].bitcast(I32))
+        identity = tile([P, P], F32, "identity")
+        make_identity(nc, identity[:])
+        nc.gpsimd.dma_start(lam_sb[:], lam)
+        nc.gpsimd.dma_start(reserve_sb[:], reserve)
+        nc.vector.memset(placed[:], 0.0)
+
+        q_bf = tile([P, Q, PACK], BF16, "q_bf")
+        q_codes = tile([P, Q], U32, "q_codes")
+        q_scales = tile([P, Q], U8, "q_scales")
+        nc.vector.tensor_copy(q_bf[:], q_raw[:].rearrange("p j w -> p w j"))
+        kw_all = tile([P, T], U32, "kw_all", "keys")
+        nc.sync.dma_start(kw_all[:].bitcast(I32), keys_words[0].rearrange("p n t -> p (n t)").bitcast(I32))
+        g_bf = tile([P, Q, PACK], BF16, "g_bf")
+        g_codes = tile([P, Q], U32, "g_codes")
+        g_scales = tile([P, Q], U8, "g_scales")
+        nc.scalar.copy(g_bf[:], g_raw[:].rearrange("p j w -> p w j"))
+        vw_all = tile([P, T], U32, "vw_all", "vals")
+        nc.sync.dma_start(vw_all[:].bitcast(I32), vals_words[0].rearrange("p n t -> p (n t)").bitcast(I32))
+        nc.vector.quantize_mx(q_codes[:].bitcast(FP8X4), q_scales[:], q_bf[:].rearrange("p w j -> p (w j)"))
+        nc.vector.quantize_mx(g_codes[:].bitcast(FP8X4), g_scales[:], g_bf[:].rearrange("p w j -> p (w j)"))
+
+        ks = tile([P, SLOTS], U8, "ks")
+        vs = tile([P, SLOTS], U8, "vs")
+        stored = tile([P, PAGES], F32, "stored")
+        nc.vector.tensor_copy(stored[:], ptab_sb[:].indirect(page_list[:]))
+        old_sb = tile([P, U], F32, "old_sb", "pages")
+        nc.sync.dma_start(old_sb[:], old)
+        nc.vector.tensor_copy(ks[:], ks_all[:].indirect(slot_list[:]))
+        nc.vector.tensor_copy(vs[:], vs_all[:].indirect(slot_list[:]))
+
+        def list_half(h):
+            return slot_list[:, h * HALF // 16:(h + 1) * HALF // 16]
+
+        def cols(h):
+            return slice(h * HALF, (h + 1) * HALF)
+
+        def by_page(ap):
+            return ap.rearrange("p (g j) -> p g j", j=PAGE)
+
+        def dealt(ap):
+            return ap.rearrange("p (g a b) -> p a g b", a=RUNS, b=RUN)
+
+        def as_runs(ap):
+            return ap.rearrange("p (a g b) -> p a g b", a=RUNS, b=RUN)
+
+        def page_sums(terms, name):
+            turned = ps.tile([P, 2, P], F32, name=name + "_turned")
+            for h in halves:
+                for a in range(RUNS):
+                    nc.tensor.matmul(turned[:, h, :], lhsT=terms[h][:, a * P:(a + 1) * P], rhs=identity[:],
+                                     is_transpose=True, start=(a == 0), stop=(a == RUNS - 1))
+            turned_sb = tile([P, 2, P], F32, name + "_turned_sb")
+            nc.scalar.copy(turned_sb[:], turned[:])
+            back = ps.tile([P, 2, P], F32, name=name + "_back")
+            for h in halves:
+                nc.tensor.transpose(back[:, h, :], turned_sb[:, h, :], identity[:])
+            sums = tile([P, PAGES], F32, name)
+            return back, sums
+
+        def finish_sums(back, sums):
+            nc.vector.tensor_reduce(sums[:], back[:].rearrange("p h (g b) -> p (h g) b", b=RUN), AX.X, ALU.add)
+
+        kw = [tile([P, HALF], U32, "kw%d" % h) for h in halves]
+        vw = [tile([P, HALF], U32, "vw%d" % h) for h in halves]
+        score = [ps.tile([P, HALF], F32, name="score%d" % h) for h in halves]
+        c0 = [ps.tile([P, HALF], F32, name="c0_%d" % h) for h in halves]
+        for h in halves:
+            nc.vector.tensor_copy(kw[h][:], kw_all[:].indirect(list_half(h)))
+            nc.tensor.matmul_mx(score[h][:], lhsT=q_codes[:].bitcast(FP8X4), lhsT_scale=q_scales[:],
+                                rhs=kw[h][:].bitcast(FP8X4), rhs_scale=ks[:, cols(h)], start=True, stop=True)
+
+        under = [tile([P, HALF], F32, "under%d" % h) for h in halves]
+        sig = [tile([P, HALF], F32, "sig%d" % h) for h in halves]
+        rest = [tile([P, HALF], F32, "rest%d" % h) for h in halves]
+        for h in halves:
+            floor = stored[:, h * HALF_PAGES:(h + 1) * HALF_PAGES].unsqueeze(2).to_broadcast([P, HALF_PAGES, PAGE])
+            nc.vector.scalar_tensor_tensor(by_page(under[h][:]), floor, lam_sb[:], by_page(score[h][:]),
+                                           ALU.mult, ALU.subtract)
+        for h in halves:
+            nc.scalar.activation(as_runs(sig[h][:]), dealt(under[h][:]), ACT.Sigmoid, scale=-1.0)
+        for h in halves:
+            nc.scalar.activation(rest[h][:], under[h][:], ACT.Sigmoid)
+        sig_back, sig_sum = page_sums(sig, "sig_sum")
+
+        log_rest = [tile([P, HALF], F32, "log_rest%d" % h) for h in halves]
+        for h in halves:
+            nc.scalar.activation(log_rest[h][:], rest[h][:], ACT.Ln, bias=guard[:])
+
+        for h in halves:
+            nc.vector.tensor_copy(vw[h][:], vw_all[:].indirect(list_half(h)))
+            nc.tensor.matmul_mx(c0[h][:], lhsT=g_codes[:].bitcast(FP8X4), lhsT_scale=g_scales[:],
+                                rhs=vw[h][:].bitcast(FP8X4), rhs_scale=vs[VALS_ROW:P, cols(h)], start=True, stop=True)
+
+        sig_c0 = [tile([P, HALF], F32, "sig_c0_%d" % h) for h in halves]
+        for h in halves:
+            nc.vector.tensor_tensor(as_runs(sig_c0[h][:]), dealt(c0[h][:]), as_runs(sig[h][:]), ALU.mult)
+        sig_c0_back, sig_c0_sum = page_sums(sig_c0, "sig_c0_sum")
+        finish_sums(sig_back, sig_sum)
+
+        neg_part = [tile([P, HALF], F32, "neg_part%d" % h) for h in halves]
+        neg_part_sum = tile([P, 2], F32, "neg_part_sum")
+        for h in halves:
+            nc.vector.scalar_tensor_tensor(neg_part[h][:], log_rest[h][:], 1.0, under[h][:], ALU.mult, ALU.min,
+                                           accum_out=neg_part_sum[:, h:h + 1])
+        neg_z = tile([P, 1], F32, "neg_z")
+        neg_inv_z = tile([P, 1], F32, "neg_inv_z")
+        factor = tile([P, 1], F32, "factor")
+        nc.vector.tensor_scalar(neg_z[:], neg_part_sum[:, 0:1], neg_part_sum[:, 1:2], reserve_sb[:], ALU.add, ALU.subtract)
+        weighted = [tile([P, HALF], F32, "weighted%d" % h) for h in halves]
+        neg_read = tile([P, 2], F32, "neg_read")
+        nc.vector.scalar_tensor_tensor(weighted[0][:], c0[0][:], 1.0, neg_part[0][:], ALU.mult, ALU.mult,
+                                       accum_out=neg_read[:, 0:1])
+        nc.vector.reciprocal(neg_inv_z[:], neg_z[:])
+        nc.vector.scalar_tensor_tensor(weighted[1][:], c0[1][:], 1.0, neg_part[1][:], ALU.mult, ALU.mult,
+                                       accum_out=neg_read[:, 1:2])
+        nc.vector.tensor_scalar(factor[:], neg_inv_z[:], lam_sb[:], 64.0, ALU.mult, ALU.mult)
+        finish_sums(sig_c0_back, sig_c0_sum)
+        mean_c0 = tile([P, 1], F32, "mean_c0")
+        nc.vector.tensor_scalar(mean_c0[:], neg_read[:, 0:1], neg_read[:, 1:2], neg_inv_z[:], ALU.add, ALU.mult)
+        pull = tile([P, PAGES], F32, "pull")
+        nc.vector.tensor_scalar(pull[:], sig_sum[:], mean_c0[:], -1.0, ALU.mult, ALU.mult)
+        nc.vector.tensor_tensor(placed[:].indirect(page_list[:]), sig_c0_sum[:], pull[:], ALU.add)
+
+        result = [tile([P, U // 2], F32, "result%d" % h) for h in range(2)]
+        for h, queue in enumerate((nc.sync, nc.scalar)):
+            part = slice(h * U // 2, (h + 1) * U // 2)
+            nc.vector.scalar_tensor_tensor(result[h][:], placed[:, part], factor[:], old_sb[:, part], ALU.mult, ALU.add)
+            queue.dma_start(out[:, part], result[h][:])

@@ -24,6 +24,7 @@ PAGE = SLOTS // PAGES
 HALF_PAGES = HALF // PAGE
 RUN = 4
 RUNS = PAGE // RUN
+KEYS_FIRST = 1024
 VALS_ROW = 4
 LN_GUARD = 2.0 ** -60
 
@@ -43,57 +44,60 @@ def tile_attend_bpagefloor_kernel(tc, query, keys_words, keys_scales, ptab, rese
         page_list = tile([P, PAGES // 16], U16, "page_list")
         ks_all = tile([P, T], U8, "ks_all")
         vs_all = tile([P, T], U8, "vs_all")
-        q_raw = tile([P, PACK, Q], F32, "q_raw", "keys")
-        g_raw = tile([P, PACK, Q], F32, "g_raw", "vals")
-        ptab_sb = tile([P, U], F32, "ptab_sb", "pages")
+        kw_all = tile([P, T], U32, "kw_all")
+        vw_all = tile([P, T], U32, "vw_all", "value_words")
+        q_raw = tile([P, PACK, Q], F32, "q_raw")
+        g_raw = tile([P, PACK, Q], F32, "g_raw")
+        ptab_sb = tile([P, U], F32, "ptab_sb")
+        old_sb = tile([P, U], F32, "old_sb")
         lam_sb = tile([P, 1], F32, "lam_sb")
         reserve_sb = tile([P, 1], F32, "reserve_sb")
         placed = tile([P, U], F32, "placed")
         guard = tile([P, 1], F32, "guard")
         warm = tile([P, 1], F32, "warm")
+        identity = tile([P, P], F32, "identity")
 
-        nc.vector.memset(ks_all[:].bitcast(I32), 0)
-        nc.vector.memset(vs_all[:].bitcast(I32), 0)
         nc.gpsimd.memset(guard[:], LN_GUARD)
+        nc.gpsimd.memset(vs_all[:, :T // 2].bitcast(I32), 0)
+        nc.vector.memset(ks_all[:].bitcast(I32), 0)
+        nc.vector.memset(vs_all[:, T // 2:].bitcast(I32), 0)
+        nc.vector.memset(identity[:], 0.0)
+        nc.vector.memset(placed[:], 0.0)
         nc.scalar.activation(warm[:], guard[:], ACT.Sigmoid)
 
+        def load_scale_rows(queue, plane, scales, first_row, r):
+            queue.dma_start(plane[first_row + r:P:32, :].bitcast(I32), scales[0, r:16:4, :].bitcast(I32))
+
+        make_identity(nc, identity[:], nomemset=True)
         nc.sync.dma_start(slot_list[:], offs)
         nc.sync.dma_start(q_raw[:], query.rearrange("(p j) w -> p j w", j=PACK))
-        nc.sync.dma_start(ptab_sb[:], ptab)
-        nc.sync.dma_start(g_raw[:], gout.rearrange("(p j) w -> p j w", j=PACK))
+        load_scale_rows(nc.sync, ks_all, keys_scales, 0, 0)
+        for r in range(1, 4):
+            load_scale_rows(nc.sync, ks_all, keys_scales, 0, r)
+            if r < 3:
+                load_scale_rows(nc.sync, vs_all, vals_scales, VALS_ROW, r - 1)
+        key_words = keys_words[0].rearrange("p n t -> p (n t)").bitcast(I32)
+        nc.sync.dma_start(kw_all[:, :KEYS_FIRST].bitcast(I32), key_words[:, :KEYS_FIRST])
+        for r in range(2, 4):
+            load_scale_rows(nc.sync, vs_all, vals_scales, VALS_ROW, r)
+        nc.sync.dma_start(kw_all[:, KEYS_FIRST:].bitcast(I32), key_words[:, KEYS_FIRST:])
         nc.sync.dma_start(page_list[:], offs2)
-        for r in range(4):
-            nc.sync.dma_start(ks_all[r:P:32, :].bitcast(I32), keys_scales[0, r:16:4, :].bitcast(I32))
-        for r in range(4):
-            nc.sync.dma_start(vs_all[VALS_ROW + r:P:32, :].bitcast(I32), vals_scales[0, r:16:4, :].bitcast(I32))
-        identity = tile([P, P], F32, "identity")
-        make_identity(nc, identity[:])
-        nc.gpsimd.dma_start(lam_sb[:], lam)
-        nc.gpsimd.dma_start(reserve_sb[:], reserve)
-        nc.vector.memset(placed[:], 0.0)
+        nc.sync.dma_start(ptab_sb[:], ptab)
+        nc.sync.dma_start(lam_sb[:], lam)
+        nc.sync.dma_start(g_raw[:], gout.rearrange("(p j) w -> p j w", j=PACK))
+        nc.sync.dma_start(vw_all[:].bitcast(I32), vals_words[0].rearrange("p n t -> p (n t)").bitcast(I32))
+        nc.sync.dma_start(old_sb[:], old)
+        nc.sync.dma_start(reserve_sb[:], reserve)
 
         q_bf = tile([P, Q, PACK], BF16, "q_bf")
         q_codes = tile([P, Q], U32, "q_codes")
         q_scales = tile([P, Q], U8, "q_scales")
         nc.vector.tensor_copy(q_bf[:], q_raw[:].rearrange("p j w -> p w j"))
-        kw_all = tile([P, T], U32, "kw_all", "keys")
-        nc.sync.dma_start(kw_all[:].bitcast(I32), keys_words[0].rearrange("p n t -> p (n t)").bitcast(I32))
-        g_bf = tile([P, Q, PACK], BF16, "g_bf")
-        g_codes = tile([P, Q], U32, "g_codes")
-        g_scales = tile([P, Q], U8, "g_scales")
-        nc.scalar.copy(g_bf[:], g_raw[:].rearrange("p j w -> p w j"))
-        vw_all = tile([P, T], U32, "vw_all", "vals")
-        nc.sync.dma_start(vw_all[:].bitcast(I32), vals_words[0].rearrange("p n t -> p (n t)").bitcast(I32))
         nc.vector.quantize_mx(q_codes[:].bitcast(FP8X4), q_scales[:], q_bf[:].rearrange("p w j -> p (w j)"))
-        nc.vector.quantize_mx(g_codes[:].bitcast(FP8X4), g_scales[:], g_bf[:].rearrange("p w j -> p (w j)"))
-
         ks = tile([P, SLOTS], U8, "ks")
-        vs = tile([P, SLOTS], U8, "vs")
-        stored = tile([P, PAGES], F32, "stored")
-        nc.vector.tensor_copy(stored[:], ptab_sb[:].indirect(page_list[:]))
-        old_sb = tile([P, U], F32, "old_sb", "pages")
-        nc.sync.dma_start(old_sb[:], old)
         nc.vector.tensor_copy(ks[:], ks_all[:].indirect(slot_list[:]))
+
+        vs = tile([P, SLOTS], U8, "vs")
         nc.vector.tensor_copy(vs[:], vs_all[:].indirect(slot_list[:]))
 
         def list_half(h):
@@ -111,23 +115,6 @@ def tile_attend_bpagefloor_kernel(tc, query, keys_words, keys_scales, ptab, rese
         def as_runs(ap):
             return ap.rearrange("p (a g b) -> p a g b", a=RUNS, b=RUN)
 
-        def page_sums(terms, name):
-            turned = ps.tile([P, 2, P], F32, name=name + "_turned")
-            for h in halves:
-                for a in range(RUNS):
-                    nc.tensor.matmul(turned[:, h, :], lhsT=terms[h][:, a * P:(a + 1) * P], rhs=identity[:],
-                                     is_transpose=True, start=(a == 0), stop=(a == RUNS - 1))
-            turned_sb = tile([P, 2, P], F32, name + "_turned_sb")
-            nc.scalar.copy(turned_sb[:], turned[:])
-            back = ps.tile([P, 2, P], F32, name=name + "_back")
-            for h in halves:
-                nc.tensor.transpose(back[:, h, :], turned_sb[:, h, :], identity[:])
-            sums = tile([P, PAGES], F32, name)
-            return back, sums
-
-        def finish_sums(back, sums):
-            nc.vector.tensor_reduce(sums[:], back[:].rearrange("p h (g b) -> p (h g) b", b=RUN), AX.X, ALU.add)
-
         kw = [tile([P, HALF], U32, "kw%d" % h) for h in halves]
         vw = [tile([P, HALF], U32, "vw%d" % h) for h in halves]
         score = [ps.tile([P, HALF], F32, name="score%d" % h) for h in halves]
@@ -136,6 +123,14 @@ def tile_attend_bpagefloor_kernel(tc, query, keys_words, keys_scales, ptab, rese
             nc.vector.tensor_copy(kw[h][:], kw_all[:].indirect(list_half(h)))
             nc.tensor.matmul_mx(score[h][:], lhsT=q_codes[:].bitcast(FP8X4), lhsT_scale=q_scales[:],
                                 rhs=kw[h][:].bitcast(FP8X4), rhs_scale=ks[:, cols(h)], start=True, stop=True)
+
+        stored = tile([P, PAGES], F32, "stored")
+        nc.vector.tensor_copy(stored[:], ptab_sb[:].indirect(page_list[:]))
+        g_bf = tile([P, Q, PACK], BF16, "g_bf")
+        g_codes = tile([P, Q], U32, "g_codes")
+        g_scales = tile([P, Q], U8, "g_scales")
+        nc.scalar.copy(g_bf[:], g_raw[:].rearrange("p j w -> p w j"))
+        nc.vector.quantize_mx(g_codes[:].bitcast(FP8X4), g_scales[:], g_bf[:].rearrange("p w j -> p (w j)"))
 
         under = [tile([P, HALF], F32, "under%d" % h) for h in halves]
         sig = [tile([P, HALF], F32, "sig%d" % h) for h in halves]
@@ -148,7 +143,10 @@ def tile_attend_bpagefloor_kernel(tc, query, keys_words, keys_scales, ptab, rese
             nc.scalar.activation(as_runs(sig[h][:]), dealt(under[h][:]), ACT.Sigmoid, scale=-1.0)
         for h in halves:
             nc.scalar.activation(rest[h][:], under[h][:], ACT.Sigmoid)
-        sig_back, sig_sum = page_sums(sig, "sig_sum")
+        sig_sum = tile([P, PAGES], F32, "sig_sum")
+        for h in halves:
+            nc.vector.tensor_reduce(sig_sum[:, h * HALF_PAGES:(h + 1) * HALF_PAGES],
+                                    sig[h][:].rearrange("p (a g b) -> p g a b", a=RUNS, b=RUN), AX.XY, ALU.add)
 
         log_rest = [tile([P, HALF], F32, "log_rest%d" % h) for h in halves]
         for h in halves:
@@ -160,31 +158,37 @@ def tile_attend_bpagefloor_kernel(tc, query, keys_words, keys_scales, ptab, rese
                                 rhs=vw[h][:].bitcast(FP8X4), rhs_scale=vs[VALS_ROW:P, cols(h)], start=True, stop=True)
 
         sig_c0 = [tile([P, HALF], F32, "sig_c0_%d" % h) for h in halves]
+        neg_part_both = tile([P, SLOTS], F32, "neg_part", "value_words")
+        neg_part = [neg_part_both[:, cols(h)] for h in halves]
+        neg_part_sum = tile([P, 2], F32, "neg_part_sum")
+        back = ps.tile([P, 2, P], F32, name="back")
         for h in halves:
             nc.vector.tensor_tensor(as_runs(sig_c0[h][:]), dealt(c0[h][:]), as_runs(sig[h][:]), ALU.mult)
-        sig_c0_back, sig_c0_sum = page_sums(sig_c0, "sig_c0_sum")
-        finish_sums(sig_back, sig_sum)
-
-        neg_part = [tile([P, HALF], F32, "neg_part%d" % h) for h in halves]
-        neg_part_sum = tile([P, 2], F32, "neg_part_sum")
-        for h in halves:
-            nc.vector.scalar_tensor_tensor(neg_part[h][:], log_rest[h][:], 1.0, under[h][:], ALU.mult, ALU.min,
+            nc.vector.scalar_tensor_tensor(neg_part[h], log_rest[h][:], 1.0, under[h][:], ALU.mult, ALU.min,
                                            accum_out=neg_part_sum[:, h:h + 1])
+            turned = ps.tile([P, P], F32, name="turned%d" % h)
+            for a in range(RUNS):
+                nc.tensor.matmul(turned[:], lhsT=sig_c0[h][:, a * P:(a + 1) * P], rhs=identity[:],
+                                 is_transpose=True, start=(a == 0), stop=(a == RUNS - 1))
+            turned_sb = tile([P, P], F32, "turned_sb%d" % h)
+            nc.scalar.copy(turned_sb[:], turned[:])
+            nc.tensor.transpose(back[:, h, :], turned_sb[:], identity[:])
         neg_z = tile([P, 1], F32, "neg_z")
         neg_inv_z = tile([P, 1], F32, "neg_inv_z")
         factor = tile([P, 1], F32, "factor")
         nc.vector.tensor_scalar(neg_z[:], neg_part_sum[:, 0:1], neg_part_sum[:, 1:2], reserve_sb[:], ALU.add, ALU.subtract)
         weighted = [tile([P, HALF], F32, "weighted%d" % h) for h in halves]
         neg_read = tile([P, 2], F32, "neg_read")
-        nc.vector.scalar_tensor_tensor(weighted[0][:], c0[0][:], 1.0, neg_part[0][:], ALU.mult, ALU.mult,
+        nc.vector.scalar_tensor_tensor(weighted[0][:], c0[0][:], 1.0, neg_part[0], ALU.mult, ALU.mult,
                                        accum_out=neg_read[:, 0:1])
         nc.vector.reciprocal(neg_inv_z[:], neg_z[:])
-        nc.vector.scalar_tensor_tensor(weighted[1][:], c0[1][:], 1.0, neg_part[1][:], ALU.mult, ALU.mult,
+        nc.vector.scalar_tensor_tensor(weighted[1][:], c0[1][:], 1.0, neg_part[1], ALU.mult, ALU.mult,
                                        accum_out=neg_read[:, 1:2])
         nc.vector.tensor_scalar(factor[:], neg_inv_z[:], lam_sb[:], 64.0, ALU.mult, ALU.mult)
-        finish_sums(sig_c0_back, sig_c0_sum)
         mean_c0 = tile([P, 1], F32, "mean_c0")
         nc.vector.tensor_scalar(mean_c0[:], neg_read[:, 0:1], neg_read[:, 1:2], neg_inv_z[:], ALU.add, ALU.mult)
+        sig_c0_sum = tile([P, PAGES], F32, "sig_c0_sum")
+        nc.vector.tensor_reduce(sig_c0_sum[:], back[:].rearrange("p h (g b) -> p (h g) b", b=RUN), AX.X, ALU.add)
         pull = tile([P, PAGES], F32, "pull")
         nc.vector.tensor_scalar(pull[:], sig_sum[:], mean_c0[:], -1.0, ALU.mult, ALU.mult)
         nc.vector.tensor_tensor(placed[:].indirect(page_list[:]), sig_c0_sum[:], pull[:], ALU.add)

@@ -57,10 +57,10 @@ def tile_attend_bpagefloor_kernel(tc, query, keys_words, keys_scales, ptab, rese
         warm = tile([P, 1], F32, "warm")
         identity = tile([P, P], F32, "identity")
 
+        nc.gpsimd.memset(ks_all[:, :T // 2].bitcast(I32), 0)
         nc.gpsimd.memset(guard[:], LN_GUARD)
-        nc.gpsimd.memset(vs_all[:, :T // 2].bitcast(I32), 0)
-        nc.vector.memset(ks_all[:].bitcast(I32), 0)
-        nc.vector.memset(vs_all[:, T // 2:].bitcast(I32), 0)
+        nc.vector.memset(ks_all[:, T // 2:].bitcast(I32), 0)
+        nc.vector.memset(vs_all[:].bitcast(I32), 0)
         nc.vector.memset(identity[:], 0.0)
         nc.vector.memset(placed[:], 0.0)
         nc.scalar.activation(warm[:], guard[:], ACT.Sigmoid)
@@ -92,7 +92,7 @@ def tile_attend_bpagefloor_kernel(tc, query, keys_words, keys_scales, ptab, rese
         q_bf = tile([P, Q, PACK], BF16, "q_bf")
         q_codes = tile([P, Q], U32, "q_codes")
         q_scales = tile([P, Q], U8, "q_scales")
-        nc.vector.tensor_copy(q_bf[:], q_raw[:].rearrange("p j w -> p w j"))
+        nc.scalar.copy(q_bf[:], q_raw[:].rearrange("p j w -> p w j"))
         nc.vector.quantize_mx(q_codes[:].bitcast(FP8X4), q_scales[:], q_bf[:].rearrange("p w j -> p (w j)"))
         ks = tile([P, SLOTS], U8, "ks")
         nc.vector.tensor_copy(ks[:], ks_all[:].indirect(slot_list[:]))
@@ -163,7 +163,9 @@ def tile_attend_bpagefloor_kernel(tc, query, keys_words, keys_scales, ptab, rese
         neg_part_sum = tile([P, 2], F32, "neg_part_sum")
         back = ps.tile([P, 2, P], F32, name="back")
         for h in halves:
-            nc.vector.tensor_tensor(as_runs(sig_c0[h][:]), dealt(c0[h][:]), as_runs(sig[h][:]), ALU.mult)
+            for runs in (slice(0, RUNS // 2), slice(RUNS // 2, RUNS)) if h == 1 else (slice(0, RUNS),):
+                nc.vector.tensor_tensor(as_runs(sig_c0[h][:])[:, runs], dealt(c0[h][:])[:, runs],
+                                        as_runs(sig[h][:])[:, runs], ALU.mult)
             nc.vector.scalar_tensor_tensor(neg_part[h], log_rest[h][:], 1.0, under[h][:], ALU.mult, ALU.min,
                                            accum_out=neg_part_sum[:, h:h + 1])
             turned = ps.tile([P, P], F32, name="turned%d" % h)
@@ -187,10 +189,10 @@ def tile_attend_bpagefloor_kernel(tc, query, keys_words, keys_scales, ptab, rese
         nc.vector.tensor_scalar(factor[:], neg_inv_z[:], lam_sb[:], 64.0, ALU.mult, ALU.mult)
         mean_c0 = tile([P, 1], F32, "mean_c0")
         nc.vector.tensor_scalar(mean_c0[:], neg_read[:, 0:1], neg_read[:, 1:2], neg_inv_z[:], ALU.add, ALU.mult)
-        sig_c0_sum = tile([P, PAGES], F32, "sig_c0_sum")
-        nc.vector.tensor_reduce(sig_c0_sum[:], back[:].rearrange("p h (g b) -> p (h g) b", b=RUN), AX.X, ALU.add)
         pull = tile([P, PAGES], F32, "pull")
         nc.vector.tensor_scalar(pull[:], sig_sum[:], mean_c0[:], -1.0, ALU.mult, ALU.mult)
+        sig_c0_sum = tile([P, PAGES], F32, "sig_c0_sum")
+        nc.vector.tensor_reduce(sig_c0_sum[:], back[:].rearrange("p h (g b) -> p (h g) b", b=RUN), AX.X, ALU.add)
         nc.vector.tensor_tensor(placed[:].indirect(page_list[:]), sig_c0_sum[:], pull[:], ALU.add)
 
         result = [tile([P, U // 2], F32, "result%d" % h) for h in range(2)]

from contextlib import ExitStack

import concourse.mybir as mybir
from concourse.masks import make_identity

D, E, T, SLOTS, PAGES, U, Q = 512, 512, 4096, 1024, 64, 512, 128
FLOPS = 2 * Q * SLOTS * (D + E)

F32 = mybir.dt.float32
BF16 = mybir.dt.bfloat16
I32 = mybir.dt.int32
U32 = mybir.dt.uint32
U16 = mybir.dt.uint16
U8 = mybir.dt.uint8
FP8X4 = mybir.dt.float8_e4m3fn_x4
ALU = mybir.AluOpType
ACT = mybir.ActivationFunctionType
AX = mybir.AxisListType

P = 128
PACK = 4
HALF = 512
PAGE = SLOTS // PAGES
HALF_PAGES = HALF // PAGE
RUN = 4
RUNS = PAGE // RUN
KEYS_FIRST = 1024
VALS_ROW = 4
LN_GUARD = 2.0 ** -60


def tile_attend_bpagefloor_kernel(tc, query, keys_words, keys_scales, ptab, reserve, gout,
                                   vals_words, vals_scales, lam, old, offs, offs2, out):
    nc = tc.nc
    halves = range(SLOTS // HALF)
    with ExitStack() as ctx:
        sb = ctx.enter_context(tc.tile_pool(name="sb", bufs=1))
        ps = ctx.enter_context(tc.psum_pool(name="ps", bufs=1))

        def tile(shape, dtype, name, tag=None):
            return sb.tile(shape, dtype, name=name, tag=tag or name, align_bytes=64)

        slot_list = tile([P, SLOTS // 16], U16, "slot_list")
        page_list = tile([P, PAGES // 16], U16, "page_list")
        ks_all = tile([P, T], U8, "ks_all")
        vs_all = tile([P, T], U8, "vs_all")
        kw_all = tile([P, T], U32, "kw_all")
        vw_all = tile([P, T], U32, "vw_all", "value_words")
        q_raw = tile([P, PACK, Q], F32, "q_raw")
        g_raw = tile([P, PACK, Q], F32, "g_raw")
        ptab_sb = tile([P, U], F32, "ptab_sb")
        old_sb = tile([P, U], F32, "old_sb")
        lam_sb = tile([P, 1], F32, "lam_sb")
        reserve_sb = tile([P, 1], F32, "reserve_sb")
        placed = tile([P, U], F32, "placed")
        guard = tile([P, 1], F32, "guard")
        warm = tile([P, 1], F32, "warm")
        identity = tile([P, P], F32, "identity")

        nc.gpsimd.memset(ks_all[:, :T // 2].bitcast(I32), 0)
        nc.gpsimd.memset(guard[:], LN_GUARD)
        nc.vector.memset(ks_all[:, T // 2:].bitcast(I32), 0)
        nc.vector.memset(vs_all[:].bitcast(I32), 0)
        nc.vector.memset(identity[:], 0.0)
        nc.vector.memset(placed[:], 0.0)
        nc.scalar.activation(warm[:], guard[:], ACT.Sigmoid)

        def load_scale_rows(queue, plane, scales, first_row, r):
            queue.dma_start(plane[first_row + r:P:32, :].bitcast(I32), scales[0, r:16:4, :].bitcast(I32))

        make_identity(nc, identity[:], nomemset=True)
        nc.sync.dma_start(slot_list[:], offs)
        nc.sync.dma_start(q_raw[:], query.rearrange("(p j) w -> p j w", j=PACK))
        load_scale_rows(nc.sync, ks_all, keys_scales, 0, 0)
        for r in range(1, 4):
            load_scale_rows(nc.sync, ks_all, keys_scales, 0, r)
            if r < 3:
                load_scale_rows(nc.sync, vs_all, vals_scales, VALS_ROW, r - 1)
        key_words = keys_words[0].rearrange("p n t -> p (n t)").bitcast(I32)
        nc.sync.dma_start(kw_all[:, :KEYS_FIRST].bitcast(I32), key_words[:, :KEYS_FIRST])
        for r in range(2, 4):
            load_scale_rows(nc.sync, vs_all, vals_scales, VALS_ROW, r)
        nc.sync.dma_start(kw_all[:, KEYS_FIRST:].bitcast(I32), key_words[:, KEYS_FIRST:])
        nc.sync.dma_start(page_list[:], offs2)
        nc.sync.dma_start(ptab_sb[:], ptab)
        nc.sync.dma_start(lam_sb[:], lam)
        nc.sync.dma_start(g_raw[:], gout.rearrange("(p j) w -> p j w", j=PACK))
        nc.sync.dma_start(vw_all[:].bitcast(I32), vals_words[0].rearrange("p n t -> p (n t)").bitcast(I32))
        nc.sync.dma_start(old_sb[:], old)
        nc.sync.dma_start(reserve_sb[:], reserve)

        q_bf = tile([P, Q, PACK], BF16, "q_bf")
        q_codes = tile([P, Q], U32, "q_codes")
        q_scales = tile([P, Q], U8, "q_scales")
        nc.scalar.copy(q_bf[:], q_raw[:].rearrange("p j w -> p w j"))
        nc.vector.quantize_mx(q_codes[:].bitcast(FP8X4), q_scales[:], q_bf[:].rearrange("p w j -> p (w j)"))
        ks = tile([P, SLOTS], U8, "ks")
        nc.vector.tensor_copy(ks[:], ks_all[:].indirect(slot_list[:]))

        vs = tile([P, SLOTS], U8, "vs")
        nc.vector.tensor_copy(vs[:], vs_all[:].indirect(slot_list[:]))

        def list_half(h):
            return slot_list[:, h * HALF // 16:(h + 1) * HALF // 16]

        def cols(h):
            return slice(h * HALF, (h + 1) * HALF)

        def by_page(ap):
            return ap.rearrange("p (g j) -> p g j", j=PAGE)

        def dealt(ap):
            return ap.rearrange("p (g a b) -> p a g b", a=RUNS, b=RUN)

        def as_runs(ap):
            return ap.rearrange("p (a g b) -> p a g b", a=RUNS, b=RUN)

        kw = [tile([P, HALF], U32, "kw%d" % h) for h in halves]
        vw = [tile([P, HALF], U32, "vw%d" % h) for h in halves]
        score = [ps.tile([P, HALF], F32, name="score%d" % h) for h in halves]
        c0 = [ps.tile([P, HALF], F32, name="c0_%d" % h) for h in halves]
        for h in halves:
            nc.vector.tensor_copy(kw[h][:], kw_all[:].indirect(list_half(h)))
            nc.tensor.matmul_mx(score[h][:], lhsT=q_codes[:].bitcast(FP8X4), lhsT_scale=q_scales[:],
                                rhs=kw[h][:].bitcast(FP8X4), rhs_scale=ks[:, cols(h)], start=True, stop=True)

        stored = tile([P, PAGES], F32, "stored")
        nc.vector.tensor_copy(stored[:], ptab_sb[:].indirect(page_list[:]))
        g_bf = tile([P, Q, PACK], BF16, "g_bf")
        g_codes = tile([P, Q], U32, "g_codes")
        g_scales = tile([P, Q], U8, "g_scales")
        nc.scalar.copy(g_bf[:], g_raw[:].rearrange("p j w -> p w j"))
        nc.vector.quantize_mx(g_codes[:].bitcast(FP8X4), g_scales[:], g_bf[:].rearrange("p w j -> p (w j)"))

        under = [tile([P, HALF], F32, "under%d" % h) for h in halves]
        sig = [tile([P, HALF], F32, "sig%d" % h) for h in halves]
        rest = [tile([P, HALF], F32, "rest%d" % h) for h in halves]
        for h in halves:
            floor = stored[:, h * HALF_PAGES:(h + 1) * HALF_PAGES].unsqueeze(2).to_broadcast([P, HALF_PAGES, PAGE])
            nc.vector.scalar_tensor_tensor(by_page(under[h][:]), floor, lam_sb[:], by_page(score[h][:]),
                                           ALU.mult, ALU.subtract)
        for h in halves:
            nc.scalar.activation(as_runs(sig[h][:]), dealt(under[h][:]), ACT.Sigmoid, scale=-1.0)
        for h in halves:
            nc.scalar.activation(rest[h][:], under[h][:], ACT.Sigmoid)
        sig_sum = tile([P, PAGES], F32, "sig_sum")
        for h in halves:
            nc.vector.tensor_reduce(sig_sum[:, h * HALF_PAGES:(h + 1) * HALF_PAGES],
                                    sig[h][:].rearrange("p (a g b) -> p g a b", a=RUNS, b=RUN), AX.XY, ALU.add)

        log_rest = [tile([P, HALF], F32, "log_rest%d" % h) for h in halves]
        for h in halves:
            nc.scalar.activation(log_rest[h][:], rest[h][:], ACT.Ln, bias=guard[:])

        for h in halves:
            nc.vector.tensor_copy(vw[h][:], vw_all[:].indirect(list_half(h)))
            nc.tensor.matmul_mx(c0[h][:], lhsT=g_codes[:].bitcast(FP8X4), lhsT_scale=g_scales[:],
                                rhs=vw[h][:].bitcast(FP8X4), rhs_scale=vs[VALS_ROW:P, cols(h)], start=True, stop=True)

        sig_c0 = [tile([P, HALF], F32, "sig_c0_%d" % h) for h in halves]
        neg_part_both = tile([P, SLOTS], F32, "neg_part", "value_words")
        neg_part = [neg_part_both[:, cols(h)] for h in halves]
        neg_part_sum = tile([P, 2], F32, "neg_part_sum")
        back = ps.tile([P, 2, P], F32, name="back")
        for h in halves:
            for runs in (slice(0, RUNS // 2), slice(RUNS // 2, RUNS)) if h == 1 else (slice(0, RUNS),):
                nc.vector.tensor_tensor(as_runs(sig_c0[h][:])[:, runs], dealt(c0[h][:])[:, runs],
                                        as_runs(sig[h][:])[:, runs], ALU.mult)
            nc.vector.scalar_tensor_tensor(neg_part[h], log_rest[h][:], 1.0, under[h][:], ALU.mult, ALU.min,
                                           accum_out=neg_part_sum[:, h:h + 1])
            turned = ps.tile([P, P], F32, name="turned%d" % h)
            for a in range(RUNS):
                nc.tensor.matmul(turned[:], lhsT=sig_c0[h][:, a * P:(a + 1) * P], rhs=identity[:],
                                 is_transpose=True, start=(a == 0), stop=(a == RUNS - 1))
            turned_sb = tile([P, P], F32, "turned_sb%d" % h)
            nc.scalar.copy(turned_sb[:], turned[:])
            nc.tensor.transpose(back[:, h, :], turned_sb[:], identity[:])
        neg_z = tile([P, 1], F32, "neg_z")
        neg_inv_z = tile([P, 1], F32, "neg_inv_z")
        factor = tile([P, 1], F32, "factor")
        nc.vector.tensor_scalar(neg_z[:], neg_part_sum[:, 0:1], neg_part_sum[:, 1:2], reserve_sb[:], ALU.add, ALU.subtract)
        weighted = [tile([P, HALF], F32, "weighted%d" % h) for h in halves]
        neg_read = tile([P, 2], F32, "neg_read")
        nc.vector.scalar_tensor_tensor(weighted[0][:], c0[0][:], 1.0, neg_part[0], ALU.mult, ALU.mult,
                                       accum_out=neg_read[:, 0:1])
        nc.vector.reciprocal(neg_inv_z[:], neg_z[:])
        nc.vector.scalar_tensor_tensor(weighted[1][:], c0[1][:], 1.0, neg_part[1], ALU.mult, ALU.mult,
                                       accum_out=neg_read[:, 1:2])
        nc.vector.tensor_scalar(factor[:], neg_inv_z[:], lam_sb[:], 64.0, ALU.mult, ALU.mult)
        mean_c0 = tile([P, 1], F32, "mean_c0")
        nc.vector.tensor_scalar(mean_c0[:], neg_read[:, 0:1], neg_read[:, 1:2], neg_inv_z[:], ALU.add, ALU.mult)
        pull = tile([P, PAGES], F32, "pull")
        nc.vector.tensor_scalar(pull[:], sig_sum[:], mean_c0[:], -1.0, ALU.mult, ALU.mult)
        sig_c0_sum = tile([P, PAGES], F32, "sig_c0_sum")
        nc.vector.tensor_reduce(sig_c0_sum[:], back[:].rearrange("p h (g b) -> p (h g) b", b=RUN), AX.X, ALU.add)
        nc.vector.tensor_tensor(placed[:].indirect(page_list[:]), sig_c0_sum[:], pull[:], ALU.add)

        result = [tile([P, U // 2], F32, "result%d" % h) for h in range(2)]
        for h, queue in enumerate((nc.sync, nc.scalar)):
            part = slice(h * U // 2, (h + 1) * U // 2)
            nc.vector.scalar_tensor_tensor(result[h][:], placed[:, part], factor[:], old_sb[:, part], ALU.mult, ALU.add)
            queue.dma_start(out[:, part], result[h][:])
